import numpy as np, ml_dtypes
CORES = [1,5,17,21,33,37,49,53]
N = 8
BF = ml_dtypes.bfloat16
def gentries(a):
    return np.ascontiguousarray(a.reshape(8, 16, -1).transpose(0, 2, 1)).reshape(8, -1)
def gtable(e):
    e = np.asarray(e); return np.ascontiguousarray(e.reshape(8, -1, 16).transpose(0, 2, 1)).reshape(128, -1).astype(np.int32)
V, W, D, RO = 1024, 2048, 8, 3
U = N * V
def family(rng):
    share = rng.permutation(np.array([1.0, 1.0, 1.0, 0.97, 0.95, 0.9, 0.6, 0.0])).reshape(8, 1, 1)
    q = rng.choice(np.array([2, 3, 4, 6]), (8, 16, 1)); often = rng.integers(0, 256, (8, 16, 8))
    v = np.take_along_axis(often, (rng.random((8, 16, W)) * q).astype(np.int64), 2)
    return np.where(rng.random((8, 16, W)) < share, v, rng.integers(0, 256, (8, 16, W)))
def parts(rng):
    return family(rng), rng.integers(0, 4096, (N, 8, V)), rng.integers(0, U, (N, 8, D, V))
def pack(f, c, e):
    return {"fam": np.ascontiguousarray(np.broadcast_to(f.reshape(1, 128, W), (N, 128, W))).astype(np.float32).astype(BF),
            "c0": np.stack([gtable(a) for a in c]), "nb": np.stack([gtable(a.reshape(8, -1)) for a in e])}
def setup_inputs(rng):
    return pack(*parts(rng))
def setup_inputs_ties(rng):
    f, c, e = parts(rng); f[:, 8:] = f[:, :8]; g = rng.permutation(8)
    f[g[0]] = rng.integers(0, 3, (1, W)); f[g[1]] = rng.integers(1, 256)
    return pack(f, c, e)
def setup_inputs_ends(rng):
    f, c, e = parts(rng); v = np.arange(V)[None, :]; a = int(rng.integers(0, N)); b = (a + 1) % N
    for r in range(N):
        e[r, 0] = rng.choice(np.array([0, U - 1, V - 1, V]), (D, V))
        e[r, 1] = np.where(rng.random((D, V)) < 0.5, r * V + v, e[r, 1]); e[r, 2] = e[r, 2, :1]
        e[r, 3] = ((r + 1) % N) * V + rng.integers(0, V, (D, V)); e[r, 4] = (r * V + v + 1 + np.arange(D)[:, None]) & (U - 1)
    e[:, 2] = b * V + (e[:, 2] & (V - 1)); e[:, 5] = b * V + int(rng.integers(0, V)); e[a] = b * V + (e[a] & (V - 1))
    c[:, 5:7] = rng.choice(np.array([0, 1, W - 1, 4094, 4095]), (N, 2, V))
    f[5] = 100 * rng.integers(0, 3, (16, W))
    f[6] = rng.integers(0, 256); f[6, 15] = np.where(rng.random(W) < 0.3, 255, rng.integers(0, 256, W))
    f[7] = rng.choice(np.array([0, 255]), (16, W)); c[:, :, 0] = 4095; c[:, :, V - 1] = 0
    c[:, 3] = (rng.permutation(U) & 4095).reshape(N, V); c[:, 4] = rng.integers(0, 4096)
    return pack(f, c, e)
def setup_inputs_same(rng):
    f, c, e = parts(rng); g = (int(rng.integers(0, 8)) + np.arange(8)) & 7
    c[:, g[0]] = rng.integers(0, 4096); c[:, g[1]] = rng.integers(0, 4096)
    c[:, g[2]] = rng.choice(rng.integers(0, 4096, 2), (N, V)); c[:, g[3]] = rng.integers(0, 4096, (N, 1))
    for i in (g[4], g[5]): f[i] = f[i][:, (np.arange(W) >> 3) << 3]
    return pack(f, c, e)
def setup_inputs_still(rng):
    f, c, e = parts(rng); c[:] = rng.integers(0, 4096, (1, 8, 1)); g = int(rng.integers(0, 8))
    for m in (g, (g + 4) & 7):
        h = (m + 7) & 7; one = int(c[0, m, 0]); two = one ^ (W >> 1); before = int(c[0, h, 0]); after = int(c[0, (m + 1) & 7, 0])
        o = rng.permutation(U); s = np.zeros(U, np.int64); s[o[U // 2:]] = 1
        e[:, m] = o[(e[:, m] & (U // 2 - 1)) + (U // 2) * s.reshape(N, 1, V)]
        c[:, m] = np.where(s == 1, two, one).reshape(N, V)
        f[h] = rng.integers(0, 256, (16, W)); f[m] = rng.integers(0, 256, (16, W))
        f[h, :, (before + two) & (W - 1)] = f[h, :, (before + one) & (W - 1)]
        f[m, 0, (two + after) & (W - 1)] = (int(f[m, 0, (one + after) & (W - 1)]) + int(rng.integers(1, 256))) & 255
    return pack(f, c, e)
def setup_inputs_spread(rng):
    ex = rng.permutation(np.array([1.0, 2.0, 4.0, 8.0, 20.0, 60.0, 200.0, 400.0])).reshape(8, 1, 1)
    f = (256 * rng.random((8, 16, W)) ** ex).astype(np.int64); up = rng.random((8, 16, 1)) < 0.5; f = np.where(up, 255 - f, f)
    c = (4096 * rng.random((N, 8, V)) ** rng.choice(np.array([1.0, 3.0, 6.0]), (N, 8, 1))).astype(np.int64)
    e = (U * rng.random((N, 8, D, V)) ** rng.choice(np.array([1.0, 2.0, 5.0]), (N, 8, D, 1))).astype(np.int64)
    return pack(f, c, e)
def check_inputs(d):
    bad = []
    for k, lo, hi in (("c0", 0, 4095), ("nb", 0, U - 1)):
        if np.min(d[k]) < lo or np.max(d[k]) > hi: bad.append("range of " + k)
    m = np.asarray(d["fam"]).astype(np.float32)
    if not np.all((m >= 0) & (m <= 255) & (m == np.floor(m))): bad.append("numbers of fam")
    if not np.all(m == m[:1]): bad.append("fam alike on all ranks")
    return bad
def reference(fam, c0, nb):
    f = fam.astype(np.float32).astype(np.int16).reshape(N, 8, 16, W)
    c = np.stack([gentries(a) for a in c0]).astype(np.int64)
    e = np.stack([gentries(a) for a in nb]).astype(np.int64).reshape(N, 8, D, V)
    k = np.arange(D)[:, None]
    for t in range(RO):
        ct = np.ascontiguousarray(c.transpose(1, 0, 2)).reshape(8, 1, U)
        look = (ct + np.roll(ct, -1, axis=0) + 1021 * t) & (W - 1)
        nc, ne, nx = [], [], []
        for a in range(N):
            p = np.take_along_axis(f[a], look, 2)
            own = p[:, :, a * V:(a + 1) * V]
            eq = np.take_along_axis(p, e[a].reshape(8, 1, D * V), 2).reshape(8, 16, D, V) == own[:, :, None, :]
            cnt = np.add.reduce(eq, axis=2, dtype=np.int64)
            x = np.argmin(cnt, axis=1)
            new = 256 * x + np.take_along_axis(own, x[:, None, :], 1)[:, 0].astype(np.int64)
            stay = np.take_along_axis(eq, x[:, None, None, :], 1)[:, 0]
            nc.append(new); nx.append(np.take_along_axis(cnt, x[:, None, :], 1)[:, 0])
            ne.append(np.where(stay, e[a], (37 * e[a] + 101 * new[:, None, :] + 811 * k + t) & (U - 1)))
        c = np.stack(nc); e = np.stack(ne); ex = np.stack(nx)
    return {"yc": np.stack([gtable(a) for a in c]).astype(np.float32), "yn": np.stack([gtable(a.reshape(8, -1)) for a in e]).astype(np.float32),
            "yx": np.stack([gtable(a) for a in ex]).astype(np.float32)}

from concourse.bass import DstId, RemoteDMATransfer
from concourse.mybir import AluOpType, ActivationFunctionType

CH = [[4, 4], [4, 4], [8]]
AS = [[4, 8], [4, 8], [5]]
GAPS = [1, 1, 3, 3, 3, 4]
TAIL = ["u0", "u1", "u2", "u3", "u4", "l", (1, 2), (1, 1), (1, 6), (1, 7)]
FILL = [(0, 0)]
DIRECT = []
HALVES = 2
F0 = [(2, 4), (1, 2)]
T0S = [(0, 0, 64), (4, 0, 64), (2, 0, 64), (7, 0, 64), (5, 0, 32)]
T0V = [(3, 0, 64), (1, 0, 64), (6, 0, 64), (5, 32, 64)]
REP = 5

SCRATCH = {
    "ca": ("sbuf", [128, 64], "int32"), "cb": ("sbuf", [128, 64], "int32"),
    "l0": ("sbuf", [128, 64], "int32"), "l1": ("sbuf", [128, 64], "int32"),
    "fm": ("sbuf", [128, 2048 * REP], "bfloat16"),
    "eb": ("sbuf", [128, 8, 64], "int32"), "eu": ("sbuf", [128, 8, 64], "uint16"),
    "ea": ("sbuf", [128, 8, 64], "float32"), "ns": ("sbuf", [128, 8, 64], "int32"),
    "zb": ("sbuf", [128, 8, 64], "int32"), "eo": ("sbuf", [128, 8, 64], "float32"),
    "lk0": ("sbuf", [128, 512], "uint16"), "lk1": ("sbuf", [128, 512], "uint16"), "lk2": ("sbuf", [128, 512], "uint16"),
    "pa": ("sbuf", [128, 8192], "bfloat16"), "pb": ("sbuf", [128, 8192], "bfloat16"),
    "po": ("sbuf", [128, 2048], "bfloat16"),
    "eq": ("sbuf", [128, 8192], "bfloat16"), "ga": ("sbuf", [128, 8192], "bfloat16"),
    "sc0": ("sbuf", [128, 1024], "float32"), "sc1": ("sbuf", [128, 512], "float32"),
    "xs": ("sbuf", [128, 768], "float32"),
    "ki": ("sbuf", [128, 64], "int32"), "hi": ("sbuf", [128, 64], "int32"), "lo": ("sbuf", [128, 64], "int32"),
    "col": ("sbuf", [128, 64], "float32"), "ci": ("sbuf", [128, 64], "int32"), "cf": ("sbuf", [128, 64], "float32"),
    "vi": ("sbuf", [128, 128], "int32"), "vt": ("sbuf", [128, 16], "int32"), "vu": ("sbuf", [128, 128], "int32"),
    "i32": ("sbuf", [128, 128], "float32"), "i101": ("sbuf", [128, 128], "float32"),
    "ib": ("sbuf", [128, 128], "bfloat16"), "wp": ("sbuf", [128, 128], "bfloat16"),
    "w": ("sbuf", [128, 9 * 128], "float16"),
    "sh": ("sbuf", [128, 128], "float32"),
    "zm": ("sbuf", [128, 240], "float32"), "d0": ("sbuf", [128, 1024], "bfloat16"), "zer": ("sbuf", [128, 128], "bfloat16"),
    "gi": ("sbuf", [128, 4], "int32"),
    "pi": ("sbuf", [128, 4], "int32"), "pt": ("sbuf", [128, 32], "int32"), "sl": ("sbuf", [128, 8], "uint16"),
    "ka": ("psum", [128, 1024], "float32"), "kb": ("psum", [128, 512], "float32"),
    "kl": ("psum", [128, 512], "float32"), "sm": ("psum", [128, 512], "float32"),
    "dd": ("psum", [128, 512], "float32"), "ow": ("psum", [128, 1024], "float32"),
}
SEMAPHORES = (["qv", "qs", "qt", "qg", "sent"] + ["dm%d" % i for i in range(28)]
              + ["ar%d_%d_%d" % (t, q, r) for t in range(3) for q in range(3) for r in range(8)]
              + ["fw%d_%d" % (t, q) for t in range(3) for q in range(3)] + ["pn"])


def rank_program(g, core, T, topo):
    rank = T.rank_of(core)
    if rank is None:
        return
    A, F = AluOpType, ActivationFunctionType
    cores = list(T.cores)
    N = len(cores)

    def mate_rank(x):
        return [r for r in range(N) if r != x and topo.chip(cores[r]) == topo.chip(cores[x])][0]

    mine = [r for r in range(N) if topo.die(cores[r]) == topo.die(core)]
    partner = mate_rank(rank)
    other = [r for r in range(N) if topo.die(cores[r]) == topo.die(cores[partner])]
    H = len(mine)
    me, pm = mine.index(rank), other.index(partner)
    slot_rank = [mine[(me + s) % H] for s in range(H)] + [other[(pm + s) % H] for s in range(H)]
    peers = [mine[(me + s) % H] for s in range(1, H)]
    for r in peers + [partner]:
        assert topo.may_write(core, cores[r])
    off_mask = topo.mask(core, cores[peers[0]])
    on_mask = topo.mask(core, cores[partner])
    n_off = len(topo.engines(core, cores[peers[0]]))
    n_on = len(topo.engines(core, cores[partner]))

    Q = {"v": g.vector, "s": g.scalar, "t": g.tensor, "g": g, "y": g.sync}
    cnt = {"qv": 0, "qs": 0, "qt": 0, "qg": 0}
    clock = {k: {} for k in Q}
    writer, readers, bank, ext, total = {}, {}, {}, {}, {}
    ndma = [0]

    def op(q, fn, rd=(), wr=(), banks=(), kind="c"):
        need = []
        for k in rd:
            if k in ext:
                need.append(ext[k])
            else:
                need.append(writer[k])
        for k in wr:
            for d in ([writer[k]] if k in writer else []) + readers.get(k, []):
                if not (q == "t" and d[3] == "t"):
                    need.append(d)
        for b in banks:
            for e, d in bank.get(b, {}).items():
                if e != q:
                    need.append(d)
        best = {}
        for d in need:
            if clock[q].get(d[0], 0) < d[1] and (d[0] not in best or best[d[0]][1] < d[1]):
                best[d[0]] = d
        for s, d in best.items():
            if any(s2 != s and d2[2].get(s, 0) >= d[1] for s2, d2 in best.items()):
                continue
            Q[q].wait_ge(T.sem[s], d[1])
        for s, d in best.items():
            for s2, v in d[2].items():
                if clock[q].get(s2, 0) < v:
                    clock[q][s2] = v
        if kind == "r":
            fn()
            return
        if kind == "d":
            s = "dm%d" % ndma[0]
            ndma[0] += 1
            v = 16
            fn().then_inc(T.sem[s], 16)
            who = "dma"
        else:
            s = "q" + q
            cnt[s] += 1
            v = cnt[s]
            fn().then_inc(T.sem[s], 1)
            who = q
        total[s] = v
        snap = dict(clock[q])
        snap[s] = v
        d = (s, v, snap, who)
        for k in rd:
            readers.setdefault(k, []).append(d)
        for k in wr:
            writer[k] = d
            readers[k] = []
        for b in banks:
            bank.setdefault(b, {})[q] = d

    V, S, PE = g.vector, g.scalar, g.tensor

    def ts(out, in0, s1, s2, o0, o1, rd, wr, banks=()):
        if o1 is None:
            op("v", lambda: V.tensor_scalar(out, in0, s1, None, o0), rd, wr, banks)
        else:
            op("v", lambda: V.tensor_scalar(out, in0, s1, s2, o0, o1), rd, wr, banks)

    def tt(out, in0, in1, o, rd, wr, banks=()):
        op("v", lambda: V.tensor_tensor(out, in0, in1, o), rd, wr, banks)

    def cp(out, in_, rd, wr, banks=()):
        op("v", lambda: V.tensor_copy(out, in_), rd, wr, banks)

    def ms(ap, c, wr):
        op("v", lambda: V.memset(ap, c), (), wr)

    def mm(out, lhsT, rhs, start, stop, rd, wr, banks):
        op("t", lambda: PE.matmul(out, lhsT, rhs, start, stop), rd, wr, banks)

    def dst(r):
        a = topo.addr(cores[r])
        return DstId(rid=a[0], pnc=a[1])

    LK = [T.lk0, T.lk1, T.lk2]
    PT = [T.pa, T.pb]

    def pcols(t, r, a, b):
        return PT[t % 2][:, r * 1024 + a:r * 1024 + b]

    def pwin(t):
        return PT[t % 2][:, 0:8192]

    def ptok(t, rs, c0, c1):
        return [("P", t % 2, r, c) for r in rs for c in range(c0 // 8, (c1 + 7) // 8)]

    def slots(t, c0, w, s0, s1):
        return LK[t][:, 8 * c0 + s0 * w:8 * c0 + s1 * w]

    def landed(t, q, ss, name, n):
        total[name] = n
        for s in ss:
            ext[("L", t, q, s)] = (name, n, {name: n}, "x")

    def send(t, q, c0, w):
        name = "ar%d_%d_%d" % (t, q, rank)
        to = [(peers[s - 1], H - s) for s in range(1, H)]
        both = (t, q) in DIRECT
        if both:
            to = to + [(mate_rank(r), H + s) for r, s in to]
        trs = [RemoteDMATransfer(dst_ids=[dst(r) for r, s in to], dma_engine_mask=off_mask, remote_sem=T.sem[name],
                                 srcs=[slots(t, c0, w, 0, 1)], dsts=[slots(t, c0, w, s, s + 1) for r, s in to])]
        if both:
            fw = "fw%d_%d" % (t, q)
            trs.append(RemoteDMATransfer(dst_ids=[dst(partner)], dma_engine_mask=on_mask & ~off_mask,
                                         remote_sem=T.sem[fw], srcs=[slots(t, c0, w, 0, 1)],
                                         dsts=[slots(t, c0, w, H, H + 1)]))
            landed(t, q, [H], fw, n_on - n_off)
        op("g", lambda: g.remote_dma_fused(trs, local_sem=T.sem.sent), [("L", t, q, 0)], kind="r")
        total["sent"] = total.get("sent", 0) + (n_on if both else n_off)
        for r, s in to:
            landed(t, q, [s], "ar%d_%d_%d" % (t, q, slot_rank[s]), n_off)

    def onchip(t, q, c0, w, s0, s1, name, mask, n):
        if (t, q) in DIRECT:
            return
        a = topo.addr(cores[partner])
        op("g", lambda: g.remote_dma(slots(t, c0, w, H + s0, H + s1), slots(t, c0, w, s0, s1), T.sem[name],
                                     T.sem.sent, a[1], a[0], mask), [("L", t, q, s) for s in range(s0, s1)], kind="r")
        total["sent"] = total.get("sent", 0) + n
        landed(t, q, range(H + s0, H + s1), name, n)

    def table(e, t, q, c0, w, s, a=0, b=None):
        b = w if b is None else b
        win = T.fm[:, 0:2048] if t == 0 else T.fm[:, 0:2048 * REP]
        ftok = ["fm0"] if t == 0 else ["fm%d" % i for i in range(REP)]
        r = slot_rank[s]
        out = pcols(t, r, 16 * (c0 + a), 16 * (c0 + b))
        off = LK[t][:, 8 * c0 + s * w + a:8 * c0 + s * w + b]
        rd = ftok + [("L", t, q, s)]
        wr = ptok(t, [r], c0 + a, c0 + b)
        if e == "v":
            cp(out, win.indirect(off), rd, wr)
        else:
            op("s", lambda: S.activation(out, win.indirect(off), F.Copy), rd, wr)
        if s == 0:
            x = 1024 * (t % 2) + 16 * c0
            op("y", lambda: g.sync.dma_start(T.po[:, x + 16 * a:x + 16 * b], out), wr,
               [("po", t % 2, c) for c in range((c0 + a) // 8, (c0 + b + 7) // 8)], kind="d")

    op("y", lambda: g.sync.dma_start(T.ca[:], T.c0[:]), (), ["ca"], kind="d")
    op("s", lambda: S.dma_start(T.cb[0:112, :], T.c0[16:128, :]), (), ["cb0"], kind="d")
    op("y", lambda: g.sync.dma_start(T.cb[112:128, :], T.c0[0:16, :]), (), ["cb1"], kind="d")
    op("y", lambda: g.sync.dma_start(T.fm[:, 0:2048], T.fam[:]), (), ["fm0"], kind="d")
    op("y", lambda: g.sync.dma_start(T.eb[:], T.nb[:]), (), ["eb"], kind="d")

    wide = max(max(c) for c in CH) * 128
    op("g", lambda: g.iota(T.vi[:], [[-1, 128]], 128, 1), (), ["vi"])
    op("g", lambda: g.iota(T.gi[:], [[128, 4]], 0, 0), (), ["gi"])
    op("g", lambda: g.iota(T.pi[:], [[0, 4]], 0, 1), (), ["pi"])
    ms(T.d0[:, 0:wide], -256.0, ["d0"])
    ms(T.zer[:], 0.0, ["zer"])
    ms(T.xs[:], 0.0, ["xs0", "xs1"])
    ms(T.zm[:], 0.0, ["zm"])
    ms(T.d0[:, 0:wide:16], 131072.0, ["d0"])
    ts(T.ib[:], T.vi[:], 128, None, A.is_equal, None, ["vi"], ["ib"])
    ts(T.vt[:], T.vi[:, 0:16], 15, None, A.bitwise_and, None, ["vi"], ["vt"])

    tt(T.l0[:], T.ca[:], T.cb[:], A.add, ["ca", "cb0", "cb1"], ["l0"])
    ts(T.l1[:], T.l0[:], 2047, None, A.bitwise_and, None, ["l0"], ["l1"])
    cp(slots(0, 0, 64, 0, 1), T.l1[:], ["l1"], [("L", 0, 0, 0)])
    send(0, 0, 0, 64)
    onchip(0, 0, 0, 64, 0, 1, "pn", on_mask & ~off_mask, n_on - n_off)
    for i, (s0, s1) in enumerate(F0):
        onchip(0, 0, 0, 64, s0, s1, "fw0_%d" % i, on_mask, n_on)

    op("s", lambda: S.activation(T.wp[:], T.ib[:], F.Copy, scale=1.0 / 256), ["ib"], ["wp"])
    op("s", lambda: S.activation(T.i32[:], T.ib[:], F.Copy), ["ib"], ["i32"])
    op("s", lambda: S.activation(T.i101[:], T.ib[:], F.Copy, scale=101.0), ["ib"], ["i101"])
    ts(T.vu[:], T.vi[:], 0x6F, None, A.bitwise_and, None, ["vi"], ["vu"])
    ts(T.zm[:, 112:128], T.vt[:], 0, None, A.is_equal, None, ["vt", "zm"], ["zm"])
    ts(T.sh[:], T.vu[:], 0, None, A.is_equal, None, ["vu"], ["sh"])
    for k in range(9):
        wk = [4096.0, -1.0][k] if k < 2 else 4096.0 - 2 ** (k - 1)
        ts(T.w[:, 128 * k:128 * k + 128], T.ib[:], wk, None, A.mult, None, ["ib"], [("w", k)])
    ts(T.pt[:, 0:4], T.pi[:], 7, None, A.bitwise_and, None, ["pi"], ["pt0"])
    ts(T.pt[:, 4:8], T.pi[:], 8, None, A.bitwise_and, None, ["pi"], ["pt1"])
    ts(T.pt[:, 8:12], T.pi[:], 1, 0x38, A.arith_shift_right, A.bitwise_and, ["pi"], ["pt2"])
    ts(T.pt[:, 16:20], T.pt[:, 4:8], 8, None, A.mult, None, ["pt1"], ["pt4"])
    tt(T.pt[:, 20:24], T.pt[:, 0:4], T.pt[:, 8:12], A.add, ["pt0", "pt2"], ["pt5"])
    tt(T.pt[:, 24:28], T.gi[:], T.pt[:, 16:20], A.add, ["gi", "pt4"], ["pt6"])
    cp(T.eu[:], T.eb[:], ["eb"], ["eu"])
    tt(T.pt[:, 28:32], T.pt[:, 20:24], T.pt[:, 24:28], A.add, ["pt5", "pt6"], ["pt7"])
    for i in range(2):
        for nj in sorted(set(CH[t][q] for t in range(3) for q in range(len(CH[t])) if CH[t][q] % 2 and q % 2 == i)):
            ms([T.sc0, T.sc1][i][:, 128 * nj:128 * nj + 128], 0.0, ["sc%d" % i])
    cp(T.sl[:, 0:4], T.pt[:, 28:32], ["pt7"], ["sl"])

    ea_all = [("ea", k) for k in range(8)]

    def linear(t):
        for k in range(8):
            ts(T.ea[:, k, :], T.eb[:, k, :], 36, 811 * k + t, A.mult, A.add, ["eb"], [("ea", k)])
        mm(T.dd[:], T.i32[:], T.ea[:], True, False, ["i32"] + ea_all, ["dd"], ["dd"])

    linear(0)
    for s, a, b in T0S:
        table("s", 0, 0, 0, 64, s, a, b)
    for s, a, b in T0V:
        table("v", 0, 0, 0, 64, s, a, b)
    for i in range(1, REP):
        op("y", lambda i=i: g.sync.dma_start(T.fm[:, 2048 * i:2048 * i + 2048], T.fam[:]),
           [("L", 0, 0, H + 1)], ["fm%d" % i], kind="d")

    allp = lambda t: ptok(t, range(N), 0, 64)
    ct_all = [("col", c) for c in range(8)]
    kt_all = [("ki", c) for c in range(8)]

    def update(last):
        D = T.dd
        st = []
        st.append(lambda: [mm(D[:, 64 * k:64 * k + 64], T.i101[:], T.col[:], False, k == 7, ["i101"] + ct_all, ["dd"], ["dd"])
                           for k in range(8)])
        st.append(lambda: [ts(T.ns[:, k, :], T.ki[:], 8 + k, 1, A.arith_shift_right, A.bitwise_and, kt_all, [("ns", k)])
                           for k in range(8)])
        if last:
            n = 8 // HALVES
            for k0 in range(0, 8, n):
                def half(k0=k0):
                    nt = [("ns", k) for k in range(k0, k0 + n)]
                    Dh = D[:, 64 * k0:64 * (k0 + n)]
                    tt(Dh, Dh, T.ns[:, k0:k0 + n, :], A.mult, ["dd"] + nt, [("dd", k0)], ["dd"])
                    tt(T.zb[:, k0:k0 + n, :], Dh, T.eb[:, k0:k0 + n, :], A.add, [("dd", k0), "eb"], [("zb", k0)], ["dd"])
                    ts(T.ns[:, k0:k0 + n, :], T.zb[:, k0:k0 + n, :], 8191, None, A.bitwise_and, None, [("zb", k0)], nt)
                    cp(T.eo[:, k0:k0 + n, :], T.ns[:, k0:k0 + n, :], nt, [("eo", k0)])
                    op("y", lambda: g.sync.dma_start(T.yn[:, 64 * k0:64 * (k0 + n)], T.eo[:, k0:k0 + n, :]),
                       [("eo", k0)], kind="d")
                st.append(half)
            return st
        st.append(lambda: tt(D[:], D[:], T.ns[:], A.mult, ["dd"] + [("ns", k) for k in range(8)], ["dd"], ["dd"]))
        st.append(lambda: tt(T.zb[:], D[:], T.eb[:], A.add, ["dd", "eb"], ["zb"], ["dd"]))
        st.append(lambda: ts(T.eb[:], T.zb[:], 8191, None, A.bitwise_and, None, ["zb"], ["eb"]))
        st.append(lambda: cp(T.eu[:], T.eb[:], ["eb"], ["eu"]))
        return st

    def keys(q, nj):
        return [(T.ka, ["ka%d" % i for i in range((nj + 3) // 4)]), (T.kb, ["kb"])][q % 2]

    def post(t, q, j0, nj, last):
        K, kb = keys(q, nj)
        SC, sb = [(T.sc0, "sc0"), (T.sc1, "sc1")][q % 2]
        n, c0, c1 = 128 * nj, 8 * j0, 8 * (j0 + nj)
        w = c1 - c0
        kt = [("ki", c) for c in range(j0, j0 + nj)]
        ct = [("col", c) for c in range(j0, j0 + nj)]

        def scan():
            op("v", lambda: V.tensor_tensor_scan(SC[:, 0:n], T.d0[:, 0:n], K[:, 0:n], 0.0, A.add, A.min),
               ["d0"] + kb, [sb], kb)

        def turn():
            h = (nj + 1) // 2
            x0 = 512 * (q % 2)
            cp(T.xs[:, x0:x0 + 128 * h].indirect(T.sl[:, 0:h]), SC[:, 15:256 * h:16], [sb, "sl"], ["xs%d" % (q % 2)])
            for gg in range(8):
                mm(T.kl[:, c0:c1], T.zm[:, 112 - 16 * gg:240 - 16 * gg], T.xs[:, x0 + gg:x0 + 64 * nj:8],
                   gg == 0, gg == 7, ["zm", "xs%d" % (q % 2)], ["kl"], ["kl"])

        def s2():
            ts(T.ki[:, c0:c1], T.kl[:, c0:c1], 256.0, 256.0 * 4095, A.mult, A.add, ["kl"], kt, ["kl"])

        def s3():
            ts(T.hi[:, c0:c1], T.ki[:, c0:c1], 8, 0xF00, A.arith_shift_right, A.bitwise_and, kt, [("hi", q)])
            ts(T.lo[:, c0:c1], T.ki[:, c0:c1], 255, None, A.bitwise_and, None, kt, [("lo", q)])

        def s4():
            tt(T.col[:, c0:c1], T.hi[:, c0:c1], T.lo[:, c0:c1], A.add, [("hi", q), ("lo", q)], ct)
            if not last:
                mm(T.sm[:, c0:c1], T.sh[:], T.col[:, c0:c1], True, True, ["sh"] + ct, ["sm"], ["sm"])

        def s5():
            ts(slots(t + 1, c0, w, 0, 1), T.sm[:, c0:c1], float(1021 * (t + 1)), None, A.add, None, ["sm"],
               [("L", t + 1, q, 0)], ["sm"])
            send(t + 1, q, c0, w)
            onchip(t + 1, q, c0, w, 0, H, "fw%d_%d" % (t + 1, q), on_mask, n_on)

        return [scan, turn, s2, s3, s4] + ([] if last else [s5])

    for t in range(3):
        last = t == 2
        ch = CH[t]
        nq = len(ch)
        starts = [sum(ch[:q]) for q in range(nq)]
        helped = [list(range(8 - AS[t][q], 8)) for q in range(nq)]
        top = max([128 * (starts[q] + ch[q]) for q in range(nq) if helped[q]] + [0])
        for a in range(0, top, 512):
            b = min(top, a + 512)
            mm(T.ow[:, a:b], T.ib[:], pcols(t, rank, a, b), True, True, ["ib"] + ptok(t, [rank], a // 16, b // 16),
               ["ow%d" % (a // 512)], ["ow%d" % (a // 512)])
        for q in range(nq):
            for k in helped[q]:
                a, b = 128 * starts[q], 128 * (starts[q] + ch[q])
                op("s", lambda k=k, a=a, b=b: S.activation(T.ga[:, 1024 * k + a:1024 * k + b],
                                                           pwin(t).indirect(T.eu[:, k, a // 16:b // 16]), F.Copy),
                   allp(t) + ["eu"], [("ga", k, j) for j in range(a // 128, b // 128)])
        pending = []
        for q in range(nq):
            j0, nj = starts[q], ch[q]
            a, b = 128 * j0, 128 * (j0 + nj)
            K, kb = keys(q, nj)
            own = ptok(t, [rank], a // 16, b // 16)
            for x in range(0, nj, 4):
                y = min(nj, x + 4)
                mm(K[:, 128 * x:128 * y], T.zer[0:32, :], T.d0[0:32, 0:128 * (y - x)], True, False, ["zer", "d0"],
                   [kb[x // 4]], [kb[x // 4]])
            for j in range(nj):
                mm(K[:, 128 * j:128 * j + 128], pcols(t, rank, a + 128 * j, a + 128 * j + 128), T.wp[:], False, False,
                   ["wp"] + own, [kb[j // 4]], [kb[j // 4]])
            direct = [k for k in range(8) if k not in helped[q]]
            order, d, h = [], list(direct), list(helped[q])
            while d or h:
                if d and (not h or (len(direct) - len(d)) * len(helped[q]) <= (len(helped[q]) - len(h)) * len(direct)):
                    order.append(d.pop(0))
                else:
                    order.append(h.pop(0))
            for i, k in enumerate(order):
                while pending and GAPS[pending[0][0]] <= i:
                    pending.pop(0)[1]()
                et = [("eq", k, j) for j in range(j0, j0 + nj)]
                out = T.eq[:, 1024 * k + a:1024 * k + b]
                if k in direct:
                    tt(out, pwin(t).indirect(T.eu[:, k, a // 16:b // 16]), T.po[:, 1024 * (t % 2) + a:1024 * (t % 2) + b],
                       A.is_equal, allp(t) + ["eu"] + [("po", t % 2, j) for j in range(j0, j0 + nj)], et)
                else:
                    ob = ["ow%d" % x for x in range(a // 512, (b - 1) // 512 + 1)]
                    tt(out, T.ga[:, 1024 * k + a:1024 * k + b], T.ow[:, a:b], A.is_equal,
                       [("ga", k, j) for j in range(j0, j0 + nj)] + ob, et, ob)
                for j in range(nj):
                    closes = i == 7 and (j % 4 == 3 or j == nj - 1)
                    for m in ([0, 1] if k == 0 else [k + 1]):
                        mm(K[:, 128 * j:128 * j + 128], T.eq[:, 1024 * k + a + 128 * j:1024 * k + a + 128 * j + 128],
                           T.w[:, 128 * m:128 * m + 128], False, closes and m != 0, [("eq", k, j0 + j), ("w", m)],
                           [kb[j // 4]], [kb[j // 4]])
            while pending:
                pending.pop(0)[1]()
            pending = list(enumerate(post(t, q, j0, nj, last)))
        while pending:
            i, st = pending.pop(0)
            st()
            if i == 1 and not last:
                for q, s in FILL:
                    table("v", t + 1, q, 8 * starts[q], 8 * ch[q], s)
        u = update(last)
        u[0]()
        if last:
            op("s", lambda: S.dma_start(T.yc[:], T.col[:]), ct_all, kind="d")
            ts(T.ci[:], T.ki[:], 20, None, A.arith_shift_right, None, kt_all, ["ci"])
            u[1]()
            cp(T.cf[:], T.ci[:], ["ci"], ["cf"])
            op("s", lambda: S.dma_start(T.yx[:], T.cf[:]), ["cf"], kind="d")
            for st in u[2:]:
                st()
        else:
            vs = set(x for x in TAIL + FILL if isinstance(x, tuple))
            down = list(range(H - 1, 0, -1))
            for q in range(nq):
                if (t + 1, q) in DIRECT:
                    seq = [0, H] + down + [H + s for s in down]
                else:
                    seq = [0] + down + list(range(H, 2 * H))
                for s in seq:
                    if (q, s) not in vs:
                        table("s", t + 1, q, 8 * starts[q], 8 * ch[q], s)
            for x in TAIL:
                if isinstance(x, tuple):
                    table("v", t + 1, x[0], 8 * starts[x[0]], 8 * ch[x[0]], x[1])
                elif x == "l":
                    linear(t + 1)
                else:
                    u[1 + int(x[1])]()

    for s, v in total.items():
        g.wait_ge(T.sem[s], v)
